import numpy as np
import ml_dtypes


def mxq(x, axis, fmt="e4m3"):
    dtype, down = {"e4m3": (ml_dtypes.float8_e4m3fn, 7), "e5m2": (ml_dtypes.float8_e5m2, 14)}[fmt]
    v = np.moveaxis(np.asarray(x, np.float32).astype(ml_dtypes.bfloat16).astype(np.float64), axis, -1)
    blocks = v.reshape(v.shape[:-1] + (-1, 32))
    amax = np.abs(blocks).max(-1, keepdims=True)
    byte = np.maximum(np.where(amax > 0, np.frexp(amax)[1] - 1 + 127, 0) - down, 1)
    scale = np.exp2(byte - 127.0)
    codes = (blocks / scale).astype(np.float32).astype(dtype).astype(np.float64)
    return np.moveaxis((codes * scale).reshape(v.shape), -1, axis)


WIDE = False


def mx_kscale(k):
    if not WIDE:
        return np.ones(k)
    levels = np.array([10, -10, 5, -5, 0])
    if k % 512:
        return np.exp2(np.random.permutation(np.resize(levels, k // 32))).repeat(32)
    a = np.empty((k // 512, 16))
    for p in range(k // 512):
        a[p, :8] = np.random.permutation(np.resize(levels, 8))
        for g in range(8):
            far = levels[np.abs(levels - a[p, g]) >= 10]
            a[p, g + 8] = far[np.random.randint(len(far))]
    return np.exp2(a.ravel()).repeat(32)


def f64(x):
    return np.asarray(x).astype(np.float64)


def striped(idx):
    return np.tile(idx.reshape(-1, 16).T, (8, 1)).astype(np.uint16)


def unstriped(offs):
    return offs[:16].T.reshape(-1).astype(np.int64)


E2M1 = np.array([0.0, 0.5, 1.0, 1.5, 2.0, 3.0, 4.0, 6.0, -0.0, -0.5, -1.0, -1.5, -2.0, -3.0, -4.0, -6.0])


def pack_weight(w, fmt):
    k, n = w.shape
    w = f64(np.asarray(w, np.float32).astype(ml_dtypes.bfloat16)).reshape(k // 32, 32, n)
    amax = np.abs(w).max(1)
    if fmt == "e4m3":
        byte = np.frexp(amax)[1] - 1 + 127 - 7
    else:
        mant, ex = np.frexp(amax / 6.0)
        byte = np.where(mant > 0.5, ex, ex - 1) + 127
    byte = np.clip(np.where(amax > 0, byte, 1), 1, 254)
    scaled = (w * np.exp2(127.0 - byte)[:, None, :]).reshape(k, n).astype(np.float32)
    by_word = np.ascontiguousarray(scaled.reshape(k // 512, 128, 4, n).transpose(0, 1, 3, 2))
    if fmt == "e4m3":
        words = by_word.astype(ml_dtypes.float8_e4m3fn).view(np.uint8)
    else:
        c = by_word.astype(ml_dtypes.float4_e2m1fn).view(np.uint8) & 0xF
        words = (c[..., 0::2] | (c[..., 1::2] << 4)).reshape(k // 512, 128, 2 * n)
    return np.ascontiguousarray(words), np.ascontiguousarray(byte.astype(np.uint8).reshape(k // 512, 16, n))


def unpack_weight(words, scales, fmt):
    g, _, n = scales.shape
    words = np.ascontiguousarray(words).reshape(g, 128, n, -1)
    if fmt == "e4m3":
        vals = words.view(ml_dtypes.float8_e4m3fn).astype(np.float64)
    else:
        nib = np.empty((g, 128, n, 4), np.uint8)
        nib[..., 0::2] = words & 0xF
        nib[..., 1::2] = words >> 4
        vals = E2M1[nib]
    vals = vals * np.repeat(np.exp2(scales.astype(np.float64) - 127.0), 8, axis=1)[..., None]
    return vals.transpose(0, 1, 3, 2).reshape(g * 512, n)


def gelu(v):
    return 0.5 * v * (1.0 + np.tanh(np.sqrt(2.0 / np.pi) * (v + 0.044715 * v**3)))


K, KA, H, S, T, S2, T3 = 1024, 512, 1024, 512, 2048, 512, 1024

def setup_inputs():
    n = np.random.standard_normal
    s = mx_kscale(K)[:, None]
    u = mx_kscale(H)[:, None]
    tab_words, tab_scales = pack_weight(n((K, T)) * s, "e4m3")
    tab2_words, tab2_scales = pack_weight(n((H, T3)) / np.sqrt(H) / u, "e4m3")
    tab3_words, tab3_scales = pack_weight(n((H, T3)) / np.sqrt(H) / u, "e4m3")
    w1 = (1.5 * n((KA, H)) / np.sqrt(K) / s[:KA]).astype(np.float32)
    w4_words, w4_scales = pack_weight(1.5 * n((K - KA, H)) / np.sqrt(K) / s[KA:], "e2m1")
    return {
        "tab_words": tab_words, "tab_scales": tab_scales,
        "offs": striped(np.random.permutation(T)[:S]),
        "tab2_words": tab2_words, "tab2_scales": tab2_scales,
        "offs2": striped(np.random.permutation(T3)[:S2]),
        "tab3_words": tab3_words, "tab3_scales": tab3_scales,
        "offs3": striped(np.random.permutation(T3)[:S2]),
        "w1": w1, "w4_words": w4_words, "w4_scales": w4_scales,
        "res": (0.7 * n((H, S))).astype(np.float32),
        "gain": (np.exp(0.3 * n(H)) * u[:, 0]).astype(np.float32),
        "scale": np.exp(0.4 * n(S2)).astype(np.float32),
    }

def reference(tab_words, tab_scales, offs, tab2_words, tab2_scales, offs2, tab3_words, tab3_scales, offs3,
              w1, w4_words, w4_scales, res, gain, scale):
    v = unpack_weight(tab_words, tab_scales, "e4m3")[:, unstriped(offs)]
    v2 = unpack_weight(tab2_words, tab2_scales, "e4m3")[:, unstriped(offs2)]
    v3 = unpack_weight(tab3_words, tab3_scales, "e4m3")[:, unstriped(offs3)]
    w1q = mxq(f64(w1), 0, "e4m3")
    w4q = unpack_weight(w4_words, w4_scales, "e2m1")
    x = w1q.T @ v[:KA] + w4q.T @ v[KA:]
    h = (np.tanh(x) + f64(res)) * f64(gain)[:, None]
    hq = mxq(h, 0, "e4m3")
    e2 = v2.T @ hq
    e3 = v3.T @ hq
    return np.maximum(e2, e3) * f64(scale)[:, None]

@@ -1,0 +1,313 @@
+from contextlib import ExitStack
+
+import concourse.mybir as mybir
+from concourse.masks import make_identity
+
+F32 = mybir.dt.float32
+BF16 = mybir.dt.bfloat16
+I32 = mybir.dt.int32
+U32 = mybir.dt.uint32
+U16 = mybir.dt.uint16
+U8 = mybir.dt.uint8
+FP8X4 = mybir.dt.float8_e4m3fn_x4
+FP4X4 = mybir.dt.float4_e2m1fn_x4
+ACT = mybir.ActivationFunctionType
+ALU = mybir.AluOpType
+
+P = 128
+K, H, S, T, S2, T3 = 1024, 1024, 512, 2048, 512, 1024
+CHUNK = 256
+CHUNKS = H // CHUNK
+HALF = 256
+FLOPS = 2 * K * H * S + 2 * 2 * H * S2 * S
+
+
+def tile_list_home_swap_score_kernel(
+    tc, tab_words, tab_scales, offs, tab2_words, tab2_scales, offs2, tab3_words, tab3_scales, offs3,
+    w1, w4_words, w4_scales, res, gain, scale, out,
+):
+    nc = tc.nc
+    with ExitStack() as ctx:
+        keep = ctx.enter_context(tc.tile_pool(name="keep", bufs=1))
+        psum = ctx.enter_context(tc.psum_pool(name="psum", bufs=8))
+
+        def sb(name, shape, dtype):
+            return keep.tile(shape, dtype, name=name, align_bytes=64)
+
+        def bank(shape):
+            return psum.tile(shape, F32, name="bank")
+
+        lists = [sb("list%d" % n, [P, S // 16], U16) for n in range(3)]
+        widths = [T, T3, T3]
+        table_words = [[sb("words%d_%d" % (n, a), [P, widths[n]], U32) for a in range(2)] for n in range(3)]
+        table_scales = [sb("scales%d" % n, [P, widths[n]], U8) for n in range(3)]
+        picked_words = [[sb("picked%d_%d" % (n, a), [P, S], U32) for a in range(2)] for n in range(3)]
+        picked_scales = [sb("picked_scales%d" % n, [P, S], U8) for n in range(3)]
+        w4_codes = sb("w4_codes", [P, 2 * H], U8)
+        w4_plane = sb("w4_plane", [P, H], U8)
+        w1_raw = [sb("w1_raw%d" % c, [P, 4, CHUNK], F32) for c in range(CHUNKS)]
+        res_raw = [sb("res_raw%d" % c, [P, 2, S], F32) for c in range(CHUNKS)]
+        gain_cols = sb("gain_cols", [P, 2, 4], F32)
+        gain_rows = sb("gain_rows", [P, H], F32)
+        scale_cols = sb("scale_cols", [P, S2 // P], F32)
+        ident = sb("ident", [P, P], F32)
+
+        nc.vector.memset(table_scales[0][:].bitcast(I32), 0)
+        nc.vector.memset(w4_plane[:].bitcast(I32), 0)
+        nc.gpsimd.memset(table_scales[1][:].bitcast(I32), 0)
+        nc.gpsimd.memset(table_scales[2][:].bitcast(I32), 0)
+        make_identity(nc, ident[:])
+
+        dram_words = [tab_words, tab2_words, tab3_words]
+        dram_scales = [tab_scales, tab2_scales, tab3_scales]
+        dram_lists = [offs, offs2, offs3]
+
+        def load_list(n):
+            nc.sync.dma_start(lists[n][:], dram_lists[n])
+
+        def load_words(n, a):
+            nc.sync.dma_start(
+                out=table_words[n][a][:].bitcast(I32),
+                in_=dram_words[n][a].rearrange("p t i -> p (t i)").bitcast(I32),
+            )
+
+        def load_tab_scales(a, q):
+            first = 32 * q + 4 * (1 - a)
+            nc.sync.dma_start(
+                out=table_scales[0][first : first + 4, :].bitcast(I32),
+                in_=tab_scales[a, 4 * q : 4 * q + 4, :].bitcast(I32),
+            )
+
+        def load_home_scales(n, q):
+            nc.sync.dma_start(
+                out=table_scales[n][32 * q : 32 * q + 8, :].bitcast(I32),
+                in_=dram_scales[n][:, 4 * q : 4 * q + 4, :].bitcast(I32),
+            )
+
+        def load_w4_scales(q):
+            nc.sync.dma_start(
+                out=w4_plane[32 * q : 32 * q + 4, :].bitcast(I32),
+                in_=w4_scales[0, 4 * q : 4 * q + 4, :].bitcast(I32),
+            )
+
+        def load_w1(c):
+            nc.sync.dma_start(
+                out=w1_raw[c][:],
+                in_=w1.rearrange("(p i) r -> p i r", i=4)[:, :, c * CHUNK : (c + 1) * CHUNK],
+            )
+
+        def load_res(c):
+            nc.sync.dma_start(
+                out=res_raw[c][:],
+                in_=res[c * CHUNK : (c + 1) * CHUNK, :].rearrange("(b p) j -> p b j", p=P),
+            )
+
+        def gather_words(n, a):
+            nc.vector.tensor_copy(picked_words[n][a][:], table_words[n][a][:].indirect(lists[n][:]))
+
+        def gather_scales(n):
+            nc.vector.tensor_copy(picked_scales[n][:], table_scales[n][:].indirect(lists[n][:]))
+
+        load_w1(0)
+        load_words(0, 0)
+        load_list(0)
+        nc.sync.dma_start(out=gain_cols[:], in_=gain.rearrange("(a p i) -> p a i", a=2, i=4))
+        for q in range(4):
+            load_tab_scales(1, q)
+        load_words(0, 1)
+        for q in range(4):
+            load_tab_scales(0, q)
+        nc.sync.dma_start(out=w4_codes[:].bitcast(I32), in_=w4_words[0].bitcast(I32))
+        load_w4_scales(0)
+        load_w4_scales(1)
+        load_res(0)
+        load_w4_scales(2)
+        load_w4_scales(3)
+        load_w1(1)
+        load_words(1, 0)
+        load_list(1)
+        load_res(1)
+        load_home_scales(1, 0)
+        load_w1(2)
+        load_home_scales(1, 1)
+        load_home_scales(1, 2)
+        load_words(1, 1)
+        load_home_scales(1, 3)
+        load_res(2)
+        load_list(2)
+        load_w1(3)
+        load_home_scales(2, 0)
+        load_words(2, 0)
+        load_home_scales(2, 1)
+        load_res(3)
+        load_home_scales(2, 2)
+        load_home_scales(2, 3)
+        load_words(2, 1)
+        with nc.allow_non_contiguous_dma(reason="one scale value for each output row"):
+            nc.sync.dma_start(out=scale_cols[:], in_=scale.rearrange("(t p) -> p t", p=P))
+
+        w1_bf = [sb("w1_bf%d" % c, [P, CHUNK, 4], BF16) for c in range(CHUNKS)]
+        w1_codes = [sb("w1_codes%d" % c, [P, CHUNK], U32) for c in range(CHUNKS)]
+        w1_plane = [sb("w1_plane%d" % c, [P, CHUNK], U8) for c in range(CHUNKS)]
+        tanh_x = [sb("tanh_x%d" % b, [P, S], F32) for b in range(H // P)]
+        h_rows = [[sb("h_rows%d_%d" % (a, jh), [P, 2, 512], BF16) for jh in range(2)] for a in range(2)]
+        h_bf = [[sb("h_bf%d_%d" % (a, jh), [P, HALF * 4], BF16) for jh in range(2)] for a in range(2)]
+        h_codes = [[sb("h_codes%d_%d" % (a, jh), [P, HALF], U32) for jh in range(2)] for a in range(2)]
+        h_plane = [[sb("h_plane%d_%d" % (a, jh), [P, HALF], U8) for jh in range(2)] for a in range(2)]
+
+        def round_w1(c):
+            nc.scalar.copy(
+                out=w1_bf[c][:].rearrange("p (g n) i -> p g i n", n=4),
+                in_=w1_raw[c][:].rearrange("p i (g n) -> p g i n", n=4),
+            )
+
+        def quantise_w1(c):
+            nc.vector.quantize_mx(
+                out=w1_codes[c][:].bitcast(FP8X4),
+                scales=w1_plane[c][:],
+                in_=w1_bf[c][:].rearrange("p r i -> p (r i)"),
+            )
+
+        def spread_gain(a):
+            spread = bank([P, 4, P])
+            for i in range(4):
+                nc.tensor.transpose(spread[:, i, :], gain_cols[:, a, i : i + 1].to_broadcast([P, P]), ident[:])
+            nc.scalar.copy(
+                out=gain_rows[:, 512 * a : 512 * (a + 1)].rearrange("j (p i) -> j p i", i=4),
+                in_=spread[:].rearrange("j i p -> j p i"),
+            )
+
+        def first_product(c):
+            for b in range(2):
+                block = 2 * c + b
+                x = bank([P, S])
+                nc.tensor.matmul_mx(
+                    out=x[:],
+                    lhsT=w1_codes[c][:, b * P : (b + 1) * P].bitcast(FP8X4),
+                    lhsT_scale=w1_plane[c][:, b * P : (b + 1) * P],
+                    rhs=picked_words[0][0][:].bitcast(FP8X4),
+                    rhs_scale=picked_scales[0][4:P, :],
+                    start=True,
+                    stop=False,
+                )
+                nc.tensor.matmul_mx(
+                    out=x[:],
+                    lhsT=w4_codes[:, 2 * block * P : 2 * (block + 1) * P].bitcast(FP4X4),
+                    lhsT_scale=w4_plane[:, block * P : (block + 1) * P],
+                    rhs=picked_words[0][1][:].bitcast(FP8X4),
+                    rhs_scale=picked_scales[0][:],
+                    start=False,
+                    stop=True,
+                )
+                nc.scalar.activation(out=tanh_x[block][:], in_=x[:], func=ACT.Tanh)
+
+        def make_h(c, jh):
+            total = bank([P, 2, CHUNK])
+            places = [(jt, b) for b in range(2) for jt in range(2)]
+            for n, (jt, b) in enumerate(places):
+                cols = slice(jh * HALF + jt * P, jh * HALF + (jt + 1) * P)
+                nc.tensor.matmul(
+                    total[:, jt, b * P : (b + 1) * P], res_raw[c][:, b, cols], ident[:],
+                    start=(n == 0), stop=False, is_transpose=True,
+                )
+            for n, (jt, b) in enumerate(places):
+                cols = slice(jh * HALF + jt * P, jh * HALF + (jt + 1) * P)
+                nc.tensor.matmul(
+                    total[:, jt, b * P : (b + 1) * P], tanh_x[2 * c + b][:, cols], ident[:],
+                    start=False, stop=(n == len(places) - 1), is_transpose=True,
+                )
+            a, part = divmod(c, 2)
+            nc.vector.tensor_tensor(
+                out=h_rows[a][jh][:, :, part * CHUNK : (part + 1) * CHUNK],
+                in0=total[:],
+                in1=gain_rows[:, c * CHUNK : (c + 1) * CHUNK].unsqueeze(1).to_broadcast([P, 2, CHUNK]),
+                op=ALU.mult,
+            )
+
+        def turn_h(a, jh):
+            turned = bank([P, 2, 2, P])
+            for jt in range(2):
+                pairs = h_rows[a][jh][:, jt, :].bitcast(F32)
+                for u in range(2):
+                    nc.tensor.transpose(turned[:, jt, u, :], pairs[:, u : 2 * P : 2], ident[:])
+            nc.scalar.copy(
+                out=h_bf[a][jh][:].bitcast(F32).rearrange("p (t j u) -> p t j u", t=2, u=2),
+                in_=turned[:].rearrange("p t u j -> p t j u"),
+            )
+
+        def quantise_h(a, jh):
+            nc.vector.quantize_mx(out=h_codes[a][jh][:].bitcast(FP8X4), scales=h_plane[a][jh][:], in_=h_bf[a][jh][:])
+
+        def scores(n, jh, mp):
+            e = bank([P, 2, HALF])
+            for t in range(2):
+                rows = slice((2 * mp + t) * P, (2 * mp + t + 1) * P)
+                for a in range(2):
+                    nc.tensor.matmul_mx(
+                        out=e[:, t, :],
+                        lhsT=picked_words[n][a][:, rows].bitcast(FP8X4),
+                        lhsT_scale=picked_scales[n][4 * a : P, rows],
+                        rhs=h_codes[a][jh][:].bitcast(FP8X4),
+                        rhs_scale=h_plane[a][jh][:],
+                        start=(a == 0),
+                        stop=(a == 1),
+                    )
+            return e
+
+        def finish(jh, mp):
+            e2 = scores(1, jh, mp)
+            e2_sb = sb("e2_sb%d_%d" % (jh, mp), [P, 2, HALF], F32)
+            nc.scalar.copy(out=e2_sb[:], in_=e2[:])
+            e3 = scores(2, jh, mp)
+            larger = sb("larger%d_%d" % (jh, mp), [P, 2, HALF], F32)
+            nc.vector.tensor_tensor(out=larger[:], in0=e3[:], in1=e2_sb[:], op=ALU.max)
+            result = sb("result%d_%d" % (jh, mp), [P, 2, HALF], F32)
+            for t in range(2):
+                nc.vector.tensor_scalar_mul(result[:, t, :], larger[:, t, :], scale_cols[:, 2 * mp + t : 2 * mp + t + 1])
+            nc.sync.dma_start(
+                out=out[2 * mp * P : 2 * (mp + 1) * P, jh * HALF : (jh + 1) * HALF].rearrange("(t p) j -> p t j", p=P),
+                in_=result[:],
+            )
+
+        round_w1(0)
+        spread_gain(0)
+        spread_gain(1)
+        quantise_w1(0)
+        gather_words(0, 0)
+        gather_words(0, 1)
+        gather_scales(0)
+        first_product(0)
+        round_w1(1)
+        make_h(0, 0)
+        make_h(0, 1)
+        quantise_w1(1)
+        first_product(1)
+        gather_words(1, 0)
+        round_w1(2)
+        make_h(1, 0)
+        make_h(1, 1)
+        quantise_w1(2)
+        first_product(2)
+        turn_h(0, 0)
+        turn_h(0, 1)
+        gather_words(1, 1)
+        gather_scales(1)
+        round_w1(3)
+        make_h(2, 0)
+        make_h(2, 1)
+        quantise_w1(3)
+        first_product(3)
+        quantise_h(0, 0)
+        quantise_h(0, 1)
+        gather_words(2, 0)
+        gather_scales(2)
+        make_h(3, 0)
+        turn_h(1, 0)
+        make_h(3, 1)
+        turn_h(1, 1)
+        gather_words(2, 1)
+        quantise_h(1, 0)
+        quantise_h(1, 1)
+        for jh in range(2):
+            for mp in range(2):
+                finish(jh, mp)

@@ -1,7 +1,6 @@
 from contextlib import ExitStack
 
 import concourse.mybir as mybir
-from concourse.masks import make_identity
 
 F32 = mybir.dt.float32
 BF16 = mybir.dt.bfloat16
@@ -16,8 +15,7 @@ ALU = mybir.AluOpType
 
 P = 128
 K, H, S, T, S2, T3 = 1024, 1024, 512, 2048, 512, 1024
-CHUNK = 256
-CHUNKS = H // CHUNK
+PASS = 512
 HALF = 256
 FLOPS = 2 * K * H * S + 2 * 2 * H * S2 * S
 
@@ -31,8 +29,8 @@ def tile_list_home_swap_score_kernel(
         keep = ctx.enter_context(tc.tile_pool(name="keep", bufs=1))
         psum = ctx.enter_context(tc.psum_pool(name="psum", bufs=8))
 
-        def sb(name, shape, dtype):
-            return keep.tile(shape, dtype, name=name, align_bytes=64)
+        def sb(name, shape, dtype, tag=None):
+            return keep.tile(shape, dtype, name=name, tag=tag or name, align_bytes=64)
 
         def bank(shape):
             return psum.tile(shape, F32, name="bank")
@@ -41,22 +39,20 @@ def tile_list_home_swap_score_kernel(
         widths = [T, T3, T3]
         table_words = [[sb("words%d_%d" % (n, a), [P, widths[n]], U32) for a in range(2)] for n in range(3)]
         table_scales = [sb("scales%d" % n, [P, widths[n]], U8) for n in range(3)]
-        picked_words = [[sb("picked%d_%d" % (n, a), [P, S], U32) for a in range(2)] for n in range(3)]
-        picked_scales = [sb("picked_scales%d" % n, [P, S], U8) for n in range(3)]
-        w4_codes = sb("w4_codes", [P, 2 * H], U8)
-        w4_plane = sb("w4_plane", [P, H], U8)
-        w1_raw = [sb("w1_raw%d" % c, [P, 4, CHUNK], F32) for c in range(CHUNKS)]
-        res_raw = [sb("res_raw%d" % c, [P, 2, S], F32) for c in range(CHUNKS)]
+        picked_words = {}
+        picked_scales = {}
+        w4_raw = sb("w4_raw", [P, H], U16)
+        w4_raw_plane = sb("w4_raw_plane", [P, H], U8)
+        w4_codes = sb("w4_codes", [P, H], U16)
+        w1_raw = [sb("w1_raw%d" % a, [P, 4, PASS], F32) for a in range(2)]
+        res_raw = [sb("res_raw%d" % a, [P, 4, S], F32) for a in range(2)]
         gain_cols = sb("gain_cols", [P, 2, 4], F32)
-        gain_rows = sb("gain_rows", [P, H], F32)
         scale_cols = sb("scale_cols", [P, S2 // P], F32)
-        ident = sb("ident", [P, P], F32)
 
+        nc.gpsimd.memset(w4_raw_plane[:].bitcast(I32), 0)
         nc.vector.memset(table_scales[0][:].bitcast(I32), 0)
-        nc.vector.memset(w4_plane[:].bitcast(I32), 0)
-        nc.gpsimd.memset(table_scales[1][:].bitcast(I32), 0)
-        nc.gpsimd.memset(table_scales[2][:].bitcast(I32), 0)
-        make_identity(nc, ident[:])
+        nc.vector.memset(table_scales[1][:].bitcast(I32), 0)
+        nc.vector.memset(table_scales[2][:].bitcast(I32), 0)
 
         dram_words = [tab_words, tab2_words, tab3_words]
         dram_scales = [tab_scales, tab2_scales, tab3_scales]
@@ -84,230 +80,209 @@ def tile_list_home_swap_score_kernel(
                 in_=dram_scales[n][:, 4 * q : 4 * q + 4, :].bitcast(I32),
             )
 
-        def load_w4_scales(q):
+        def load_w1(a):
             nc.sync.dma_start(
-                out=w4_plane[32 * q : 32 * q + 4, :].bitcast(I32),
-                in_=w4_scales[0, 4 * q : 4 * q + 4, :].bitcast(I32),
+                out=w1_raw[a][:],
+                in_=w1.rearrange("(p i) r -> p i r", i=4)[:, :, a * PASS : (a + 1) * PASS],
             )
 
-        def load_w1(c):
+        def load_res(a):
             nc.sync.dma_start(
-                out=w1_raw[c][:],
-                in_=w1.rearrange("(p i) r -> p i r", i=4)[:, :, c * CHUNK : (c + 1) * CHUNK],
+                out=res_raw[a][:],
+                in_=res[a * PASS : (a + 1) * PASS, :].rearrange("(p t) j -> p t j", t=4),
             )
 
-        def load_res(c):
-            nc.sync.dma_start(
-                out=res_raw[c][:],
-                in_=res[c * CHUNK : (c + 1) * CHUNK, :].rearrange("(b p) j -> p b j", p=P),
-            )
+        def gather_words(n, a, tag=None):
+            picked_words[n, a] = sb("picked%d_%d" % (n, a), [P, S], U32, tag)
+            nc.vector.tensor_copy(picked_words[n, a][:], table_words[n][a][:].indirect(lists[n][:]))
 
-        def gather_words(n, a):
-            nc.vector.tensor_copy(picked_words[n][a][:], table_words[n][a][:].indirect(lists[n][:]))
-
-        def gather_scales(n):
+        def gather_scales(n, tag=None):
+            picked_scales[n] = sb("picked_scales%d" % n, [P, S], U8, tag)
             nc.vector.tensor_copy(picked_scales[n][:], table_scales[n][:].indirect(lists[n][:]))
 
-        load_w1(0)
-        load_words(0, 0)
-        load_list(0)
-        nc.sync.dma_start(out=gain_cols[:], in_=gain.rearrange("(a p i) -> p a i", a=2, i=4))
         for q in range(4):
-            load_tab_scales(1, q)
-        load_words(0, 1)
+            nc.gpsimd.dma_start(
+                out=w4_raw_plane[32 * q : 32 * q + 4, :].bitcast(I32),
+                in_=w4_scales[0, 4 * q : 4 * q + 4, :].bitcast(I32),
+            )
+        load_list(0)
+        nc.sync.dma_start(out=w4_raw[:].bitcast(I32), in_=w4_words[0].bitcast(I32))
+        load_w1(0)
         for q in range(4):
             load_tab_scales(0, q)
-        nc.sync.dma_start(out=w4_codes[:].bitcast(I32), in_=w4_words[0].bitcast(I32))
-        load_w4_scales(0)
-        load_w4_scales(1)
-        load_res(0)
-        load_w4_scales(2)
-        load_w4_scales(3)
+        load_words(0, 0)
+        load_tab_scales(1, 0)
         load_w1(1)
-        load_words(1, 0)
+        for q in range(1, 4):
+            load_tab_scales(1, q)
+        nc.sync.dma_start(out=gain_cols[:], in_=gain.rearrange("(a p t) -> p a t", a=2, t=4))
+        load_words(0, 1)
         load_list(1)
-        load_res(1)
-        load_home_scales(1, 0)
-        load_w1(2)
-        load_home_scales(1, 1)
-        load_home_scales(1, 2)
+        load_res(0)
+        for q in range(4):
+            load_home_scales(1, q)
+        load_words(1, 0)
         load_words(1, 1)
-        load_home_scales(1, 3)
-        load_res(2)
+        load_res(1)
         load_list(2)
-        load_w1(3)
-        load_home_scales(2, 0)
+        for q in range(4):
+            load_home_scales(2, q)
         load_words(2, 0)
-        load_home_scales(2, 1)
-        load_res(3)
-        load_home_scales(2, 2)
-        load_home_scales(2, 3)
         load_words(2, 1)
         with nc.allow_non_contiguous_dma(reason="one scale value for each output row"):
             nc.sync.dma_start(out=scale_cols[:], in_=scale.rearrange("(t p) -> p t", p=P))
 
-        w1_bf = [sb("w1_bf%d" % c, [P, CHUNK, 4], BF16) for c in range(CHUNKS)]
-        w1_codes = [sb("w1_codes%d" % c, [P, CHUNK], U32) for c in range(CHUNKS)]
-        w1_plane = [sb("w1_plane%d" % c, [P, CHUNK], U8) for c in range(CHUNKS)]
-        tanh_x = [sb("tanh_x%d" % b, [P, S], F32) for b in range(H // P)]
-        h_rows = [[sb("h_rows%d_%d" % (a, jh), [P, 2, 512], BF16) for jh in range(2)] for a in range(2)]
-        h_bf = [[sb("h_bf%d_%d" % (a, jh), [P, HALF * 4], BF16) for jh in range(2)] for a in range(2)]
-        h_codes = [[sb("h_codes%d_%d" % (a, jh), [P, HALF], U32) for jh in range(2)] for a in range(2)]
+        w1_bf = {}
+        w1_codes = [sb("w1_codes%d" % a, [P, PASS], U32) for a in range(2)]
+        w1_plane = [sb("w1_plane%d" % a, [P, PASS], U8) for a in range(2)]
+        tanh_x = [[sb("tanh_x%d_%d" % (a, t), [P, S], F32) for t in range(4)] for a in range(2)]
+        res_gain = [[sb("res_gain%d_%d" % (a, t), [P, S], F32) for t in range(4)] for a in range(2)]
+        h_planes = [sb("h_planes%d" % a, [P, 4, S], BF16) for a in range(2)]
+        h_bf = [[sb("h_bf%d_%d" % (a, jh), [P, HALF, 4], BF16) for jh in range(2)] for a in range(2)]
+        h_codes = {}
         h_plane = [[sb("h_plane%d_%d" % (a, jh), [P, HALF], U8) for jh in range(2)] for a in range(2)]
 
-        def round_w1(c):
-            nc.scalar.copy(
-                out=w1_bf[c][:].rearrange("p (g n) i -> p g i n", n=4),
-                in_=w1_raw[c][:].rearrange("p i (g n) -> p g i n", n=4),
+        def deal_columns(dealt, raw):
+            nc.vector.tensor_copy(
+                out=dealt[:].rearrange("p (a t m) -> p a t m", a=2, t=4),
+                in_=raw[:].rearrange("p (a m t) -> p a t m", a=2, t=4),
             )
 
-        def quantise_w1(c):
+        def round_w1(a):
+            w1_bf[a] = sb("w1_bf%d" % a, [P, 4, P, 4], BF16)
+            nc.scalar.copy(
+                out=w1_bf[a][:].rearrange("p t m i -> p m i t"),
+                in_=w1_raw[a][:].rearrange("p i (m t) -> p m i t", t=4),
+            )
+
+        def quantise_w1(a):
             nc.vector.quantize_mx(
-                out=w1_codes[c][:].bitcast(FP8X4),
-                scales=w1_plane[c][:],
-                in_=w1_bf[c][:].rearrange("p r i -> p (r i)"),
+                out=w1_codes[a][:].bitcast(FP8X4),
+                scales=w1_plane[a][:],
+                in_=w1_bf[a][:].rearrange("p t m i -> p (t m i)"),
             )
 
-        def spread_gain(a):
-            spread = bank([P, 4, P])
-            for i in range(4):
-                nc.tensor.transpose(spread[:, i, :], gain_cols[:, a, i : i + 1].to_broadcast([P, P]), ident[:])
-            nc.scalar.copy(
-                out=gain_rows[:, 512 * a : 512 * (a + 1)].rearrange("j (p i) -> j p i", i=4),
-                in_=spread[:].rearrange("j i p -> j p i"),
-            )
-
-        def first_product(c):
-            for b in range(2):
-                block = 2 * c + b
+        def first_product(a):
+            for t in range(4):
+                cols = slice(t * P, (t + 1) * P)
+                w4_cols = slice(a * PASS + t * P, a * PASS + (t + 1) * P)
                 x = bank([P, S])
                 nc.tensor.matmul_mx(
                     out=x[:],
-                    lhsT=w1_codes[c][:, b * P : (b + 1) * P].bitcast(FP8X4),
-                    lhsT_scale=w1_plane[c][:, b * P : (b + 1) * P],
-                    rhs=picked_words[0][0][:].bitcast(FP8X4),
+                    lhsT=w1_codes[a][:, cols].bitcast(FP8X4),
+                    lhsT_scale=w1_plane[a][:, cols],
+                    rhs=picked_words[0, 0][:].bitcast(FP8X4),
                     rhs_scale=picked_scales[0][4:P, :],
                     start=True,
                     stop=False,
                 )
                 nc.tensor.matmul_mx(
                     out=x[:],
-                    lhsT=w4_codes[:, 2 * block * P : 2 * (block + 1) * P].bitcast(FP4X4),
-                    lhsT_scale=w4_plane[:, block * P : (block + 1) * P],
-                    rhs=picked_words[0][1][:].bitcast(FP8X4),
+                    lhsT=w4_codes[:, w4_cols].bitcast(FP4X4),
+                    lhsT_scale=w4_plane[:, w4_cols],
+                    rhs=picked_words[0, 1][:].bitcast(FP8X4),
                     rhs_scale=picked_scales[0][:],
                     start=False,
                     stop=True,
                 )
-                nc.scalar.activation(out=tanh_x[block][:], in_=x[:], func=ACT.Tanh)
+                nc.scalar.activation(out=tanh_x[a][t][:], in_=x[:], func=ACT.Tanh)
 
-        def make_h(c, jh):
-            total = bank([P, 2, CHUNK])
-            places = [(jt, b) for b in range(2) for jt in range(2)]
-            for n, (jt, b) in enumerate(places):
-                cols = slice(jh * HALF + jt * P, jh * HALF + (jt + 1) * P)
-                nc.tensor.matmul(
-                    total[:, jt, b * P : (b + 1) * P], res_raw[c][:, b, cols], ident[:],
-                    start=(n == 0), stop=False, is_transpose=True,
+        def scale_res(a, on_vector):
+            for t in range(4):
+                if on_vector:
+                    nc.vector.tensor_scalar_mul(res_gain[a][t][:], res_raw[a][:, t, :], gain_cols[:, a, t : t + 1])
+                else:
+                    nc.scalar.activation(
+                        out=res_gain[a][t][:], in_=res_raw[a][:, t, :], func=ACT.Copy, scale=gain_cols[:, a, t : t + 1]
+                    )
+
+        def make_h(a):
+            for t in range(4):
+                nc.vector.scalar_tensor_tensor(
+                    out=h_planes[a][:, t, :], in0=tanh_x[a][t][:], scalar=gain_cols[:, a, t : t + 1],
+                    in1=res_gain[a][t][:], op0=ALU.mult, op1=ALU.add,
                 )
-            for n, (jt, b) in enumerate(places):
-                cols = slice(jh * HALF + jt * P, jh * HALF + (jt + 1) * P)
-                nc.tensor.matmul(
-                    total[:, jt, b * P : (b + 1) * P], tanh_x[2 * c + b][:, cols], ident[:],
-                    start=False, stop=(n == len(places) - 1), is_transpose=True,
-                )
-            a, part = divmod(c, 2)
-            nc.vector.tensor_tensor(
-                out=h_rows[a][jh][:, :, part * CHUNK : (part + 1) * CHUNK],
-                in0=total[:],
-                in1=gain_rows[:, c * CHUNK : (c + 1) * CHUNK].unsqueeze(1).to_broadcast([P, 2, CHUNK]),
-                op=ALU.mult,
+
+        def weave_h(a, jh, copy):
+            copy(
+                out=h_bf[a][jh][:].rearrange("p (g n) t -> p g t n", n=4),
+                in_=h_planes[a][:, :, jh * HALF : (jh + 1) * HALF].rearrange("p t (g n) -> p g t n", n=4),
             )
 
-        def turn_h(a, jh):
-            turned = bank([P, 2, 2, P])
-            for jt in range(2):
-                pairs = h_rows[a][jh][:, jt, :].bitcast(F32)
-                for u in range(2):
-                    nc.tensor.transpose(turned[:, jt, u, :], pairs[:, u : 2 * P : 2], ident[:])
-            nc.scalar.copy(
-                out=h_bf[a][jh][:].bitcast(F32).rearrange("p (t j u) -> p t j u", t=2, u=2),
-                in_=turned[:].rearrange("p t u j -> p t j u"),
+        def quantise_h(a, jh, tag=None):
+            h_codes[a, jh] = sb("h_codes%d_%d" % (a, jh), [P, HALF], U32, tag)
+            nc.vector.quantize_mx(
+                out=h_codes[a, jh][:].bitcast(FP8X4),
+                scales=h_plane[a][jh][:],
+                in_=h_bf[a][jh][:].rearrange("p j t -> p (j t)"),
             )
 
-        def quantise_h(a, jh):
-            nc.vector.quantize_mx(out=h_codes[a][jh][:].bitcast(FP8X4), scales=h_plane[a][jh][:], in_=h_bf[a][jh][:])
-
-        def scores(n, jh, mp):
-            e = bank([P, 2, HALF])
+        def score_pass(e, n, jh, mp, a):
             for t in range(2):
                 rows = slice((2 * mp + t) * P, (2 * mp + t + 1) * P)
-                for a in range(2):
-                    nc.tensor.matmul_mx(
-                        out=e[:, t, :],
-                        lhsT=picked_words[n][a][:, rows].bitcast(FP8X4),
-                        lhsT_scale=picked_scales[n][4 * a : P, rows],
-                        rhs=h_codes[a][jh][:].bitcast(FP8X4),
-                        rhs_scale=h_plane[a][jh][:],
-                        start=(a == 0),
-                        stop=(a == 1),
-                    )
-            return e
+                nc.tensor.matmul_mx(
+                    out=e[:, t, :],
+                    lhsT=picked_words[n, a][:, rows].bitcast(FP8X4),
+                    lhsT_scale=picked_scales[n][4 * a : P, rows],
+                    rhs=h_codes[a, jh][:].bitcast(FP8X4),
+                    rhs_scale=h_plane[a][jh][:],
+                    start=(a == 0 and t == 0),
+                    stop=(a == 1 and t == 1),
+                )
 
-        def finish(jh, mp):
-            e2 = scores(1, jh, mp)
+        def finish(e2, e3, jh, mp):
+            score_pass(e2, 1, jh, mp, 1)
             e2_sb = sb("e2_sb%d_%d" % (jh, mp), [P, 2, HALF], F32)
             nc.scalar.copy(out=e2_sb[:], in_=e2[:])
-            e3 = scores(2, jh, mp)
+            score_pass(e3, 2, jh, mp, 1)
             larger = sb("larger%d_%d" % (jh, mp), [P, 2, HALF], F32)
             nc.vector.tensor_tensor(out=larger[:], in0=e3[:], in1=e2_sb[:], op=ALU.max)
             result = sb("result%d_%d" % (jh, mp), [P, 2, HALF], F32)
-            for t in range(2):
-                nc.vector.tensor_scalar_mul(result[:, t, :], larger[:, t, :], scale_cols[:, 2 * mp + t : 2 * mp + t + 1])
+            nc.gpsimd.tensor_scalar(
+                out=result[:, 0, :], in0=larger[:, 0, :],
+                scalar1=scale_cols[:, 2 * mp : 2 * mp + 1], scalar2=0.0, op0=ALU.mult, op1=ALU.add,
+            )
+            nc.vector.tensor_scalar_mul(result[:, 1, :], larger[:, 1, :], scale_cols[:, 2 * mp + 1 : 2 * mp + 2])
             nc.sync.dma_start(
                 out=out[2 * mp * P : 2 * (mp + 1) * P, jh * HALF : (jh + 1) * HALF].rearrange("(t p) j -> p t j", p=P),
                 in_=result[:],
             )
 
+        deal_columns(w4_codes, w4_raw)
         round_w1(0)
-        spread_gain(0)
-        spread_gain(1)
-        quantise_w1(0)
         gather_words(0, 0)
-        gather_words(0, 1)
-        gather_scales(0)
-        first_product(0)
+        quantise_w1(0)
+        w4_plane = sb("w4_plane", [P, H], U8, "w1_bf0")
+        deal_columns(w4_plane, w4_raw_plane)
         round_w1(1)
-        make_h(0, 0)
-        make_h(0, 1)
+        gather_scales(0)
+        gather_words(0, 1)
+        first_product(0)
         quantise_w1(1)
         first_product(1)
-        gather_words(1, 0)
-        round_w1(2)
-        make_h(1, 0)
-        make_h(1, 1)
-        quantise_w1(2)
-        first_product(2)
-        turn_h(0, 0)
-        turn_h(0, 1)
-        gather_words(1, 1)
-        gather_scales(1)
-        round_w1(3)
-        make_h(2, 0)
-        make_h(2, 1)
-        quantise_w1(3)
-        first_product(3)
+        scale_res(0, True)
+        make_h(0)
+        weave_h(0, 0, nc.vector.tensor_copy)
+        weave_h(0, 1, nc.vector.tensor_copy)
         quantise_h(0, 0)
         quantise_h(0, 1)
-        gather_words(2, 0)
-        gather_scales(2)
-        make_h(3, 0)
-        turn_h(1, 0)
-        make_h(3, 1)
-        turn_h(1, 1)
-        gather_words(2, 1)
+        scale_res(1, False)
+        gather_scales(1)
+        gather_words(1, 0)
+        gather_words(1, 1)
+        make_h(1)
+        weave_h(1, 0, nc.scalar.copy)
+        weave_h(1, 1, nc.scalar.copy)
+        gather_scales(2, "res_gain1_2")
+        gather_words(2, 0, "tanh_x1_3")
+        blocks = [(jh, mp) for jh in range(2) for mp in range(2)]
+        sums = {}
+        for n in (1, 2):
+            for jh, mp in blocks:
+                sums[n, jh, mp] = bank([P, 2, HALF])
+                score_pass(sums[n, jh, mp], n, jh, mp, 0)
+        gather_words(2, 1, "res_gain1_3")
         quantise_h(1, 0)
         quantise_h(1, 1)
-        for jh in range(2):
-            for mp in range(2):
-                finish(jh, mp)
+        for jh, mp in blocks:
+            finish(sums[1, jh, mp], sums[2, jh, mp], jh, mp)

@@ -50,8 +50,8 @@ def tile_list_home_swap_score_kernel(
         scale_cols = sb("scale_cols", [P, S2 // P], F32)
 
         nc.gpsimd.memset(w4_raw_plane[:].bitcast(I32), 0)
+        nc.gpsimd.memset(table_scales[1][:].bitcast(I32), 0)
         nc.vector.memset(table_scales[0][:].bitcast(I32), 0)
-        nc.vector.memset(table_scales[1][:].bitcast(I32), 0)
         nc.vector.memset(table_scales[2][:].bitcast(I32), 0)
 
         dram_words = [tab_words, tab2_words, tab3_words]
@@ -74,8 +74,8 @@ def tile_list_home_swap_score_kernel(
                 in_=tab_scales[a, 4 * q : 4 * q + 4, :].bitcast(I32),
             )
 
-        def load_home_scales(n, q):
-            nc.sync.dma_start(
+        def load_home_scales(n, q, queue):
+            queue.dma_start(
                 out=table_scales[n][32 * q : 32 * q + 8, :].bitcast(I32),
                 in_=dram_scales[n][:, 4 * q : 4 * q + 4, :].bitcast(I32),
             )
@@ -101,39 +101,40 @@ def tile_list_home_swap_score_kernel(
             nc.vector.tensor_copy(picked_scales[n][:], table_scales[n][:].indirect(lists[n][:]))
 
         for q in range(4):
-            nc.gpsimd.dma_start(
-                out=w4_raw_plane[32 * q : 32 * q + 4, :].bitcast(I32),
-                in_=w4_scales[0, 4 * q : 4 * q + 4, :].bitcast(I32),
-            )
+            load_home_scales(1, q, nc.gpsimd)
         load_list(0)
+        load_list(1)
         nc.sync.dma_start(out=w4_raw[:].bitcast(I32), in_=w4_words[0].bitcast(I32))
         load_w1(0)
         for q in range(4):
-            load_tab_scales(0, q)
+            nc.sync.dma_start(
+                out=w4_raw_plane[32 * q : 32 * q + 4, :].bitcast(I32),
+                in_=w4_scales[0, 4 * q : 4 * q + 4, :].bitcast(I32),
+            )
         load_words(0, 0)
-        load_tab_scales(1, 0)
+        load_tab_scales(0, 0)
+        load_tab_scales(0, 1)
         load_w1(1)
-        for q in range(1, 4):
-            load_tab_scales(1, q)
-        nc.sync.dma_start(out=gain_cols[:], in_=gain.rearrange("(a p t) -> p a t", a=2, t=4))
-        load_words(0, 1)
-        load_list(1)
-        load_res(0)
+        load_tab_scales(0, 2)
+        load_tab_scales(0, 3)
         for q in range(4):
-            load_home_scales(1, q)
+            load_tab_scales(1, q)
+        load_words(0, 1)
+        load_res(0)
+        nc.sync.dma_start(out=gain_cols[:], in_=gain.rearrange("(a p t) -> p a t", a=2, t=4))
         load_words(1, 0)
         load_words(1, 1)
         load_res(1)
         load_list(2)
         for q in range(4):
-            load_home_scales(2, q)
+            load_home_scales(2, q, nc.sync)
         load_words(2, 0)
         load_words(2, 1)
         with nc.allow_non_contiguous_dma(reason="one scale value for each output row"):
             nc.sync.dma_start(out=scale_cols[:], in_=scale.rearrange("(t p) -> p t", p=P))
 
         w1_bf = {}
-        w1_codes = [sb("w1_codes%d" % a, [P, PASS], U32) for a in range(2)]
+        w1_codes = {}
         w1_plane = [sb("w1_plane%d" % a, [P, PASS], U8) for a in range(2)]
         tanh_x = [[sb("tanh_x%d_%d" % (a, t), [P, S], F32) for t in range(4)] for a in range(2)]
         res_gain = [[sb("res_gain%d_%d" % (a, t), [P, S], F32) for t in range(4)] for a in range(2)]
@@ -155,7 +156,8 @@ def tile_list_home_swap_score_kernel(
                 in_=w1_raw[a][:].rearrange("p i (m t) -> p m i t", t=4),
             )
 
-        def quantise_w1(a):
+        def quantise_w1(a, tag=None):
+            w1_codes[a] = sb("w1_codes%d" % a, [P, PASS], U32, tag)
             nc.vector.quantize_mx(
                 out=w1_codes[a][:].bitcast(FP8X4),
                 scales=w1_plane[a][:],
@@ -187,9 +189,9 @@ def tile_list_home_swap_score_kernel(
                 )
                 nc.scalar.activation(out=tanh_x[a][t][:], in_=x[:], func=ACT.Tanh)
 
-        def scale_res(a, on_vector):
+        def scale_res(a, vector_planes):
             for t in range(4):
-                if on_vector:
+                if t < vector_planes:
                     nc.vector.tensor_scalar_mul(res_gain[a][t][:], res_raw[a][:, t, :], gain_cols[:, a, t : t + 1])
                 else:
                     nc.scalar.activation(
@@ -230,19 +232,24 @@ def tile_list_home_swap_score_kernel(
                     stop=(a == 1 and t == 1),
                 )
 
-        def finish(e2, e3, jh, mp):
+        def close_e2(e2, jh, mp):
             score_pass(e2, 1, jh, mp, 1)
             e2_sb = sb("e2_sb%d_%d" % (jh, mp), [P, 2, HALF], F32)
             nc.scalar.copy(out=e2_sb[:], in_=e2[:])
+            return e2_sb
+
+        def finish(e2_sb, e3, jh, mp):
             score_pass(e3, 2, jh, mp, 1)
             larger = sb("larger%d_%d" % (jh, mp), [P, 2, HALF], F32)
             nc.vector.tensor_tensor(out=larger[:], in0=e3[:], in1=e2_sb[:], op=ALU.max)
             result = sb("result%d_%d" % (jh, mp), [P, 2, HALF], F32)
-            nc.gpsimd.tensor_scalar(
-                out=result[:, 0, :], in0=larger[:, 0, :],
-                scalar1=scale_cols[:, 2 * mp : 2 * mp + 1], scalar2=0.0, op0=ALU.mult, op1=ALU.add,
+            nc.scalar.activation(
+                out=result[:, 0, :], in_=larger[:, 0, :], func=ACT.Copy, scale=scale_cols[:, 2 * mp : 2 * mp + 1]
             )
-            nc.vector.tensor_scalar_mul(result[:, 1, :], larger[:, 1, :], scale_cols[:, 2 * mp + 1 : 2 * mp + 2])
+            nc.gpsimd.tensor_scalar(
+                out=result[:, 1, :], in0=larger[:, 1, :],
+                scalar1=scale_cols[:, 2 * mp + 1 : 2 * mp + 2], scalar2=0.0, op0=ALU.mult, op1=ALU.add,
+            )
             nc.sync.dma_start(
                 out=out[2 * mp * P : 2 * (mp + 1) * P, jh * HALF : (jh + 1) * HALF].rearrange("(t p) j -> p t j", p=P),
                 in_=result[:],
@@ -250,39 +257,40 @@ def tile_list_home_swap_score_kernel(
 
         deal_columns(w4_codes, w4_raw)
         round_w1(0)
+        w4_plane = sb("w4_plane", [P, H], U8)
+        deal_columns(w4_plane, w4_raw_plane)
         gather_words(0, 0)
         quantise_w1(0)
-        w4_plane = sb("w4_plane", [P, H], U8, "w1_bf0")
-        deal_columns(w4_plane, w4_raw_plane)
         round_w1(1)
         gather_scales(0)
+        gather_scales(1, "scales0")
         gather_words(0, 1)
         first_product(0)
-        quantise_w1(1)
+        quantise_w1(1, "words0_1")
         first_product(1)
-        scale_res(0, True)
+        scale_res(0, 4)
         make_h(0)
-        weave_h(0, 0, nc.vector.tensor_copy)
-        weave_h(0, 1, nc.vector.tensor_copy)
-        quantise_h(0, 0)
-        quantise_h(0, 1)
-        scale_res(1, False)
-        gather_scales(1)
+        scale_res(1, 2)
+        weave_h(0, 0, nc.scalar.copy)
+        weave_h(0, 1, nc.scalar.copy)
         gather_words(1, 0)
         gather_words(1, 1)
         make_h(1)
         weave_h(1, 0, nc.scalar.copy)
         weave_h(1, 1, nc.scalar.copy)
-        gather_scales(2, "res_gain1_2")
-        gather_words(2, 0, "tanh_x1_3")
+        quantise_h(0, 0, "tanh_x1_2")
+        quantise_h(0, 1, "res_gain1_2")
+        gather_scales(2, "h_bf0_0")
+        gather_words(2, 0, "h_bf0_1")
         blocks = [(jh, mp) for jh in range(2) for mp in range(2)]
         sums = {}
         for n in (1, 2):
             for jh, mp in blocks:
                 sums[n, jh, mp] = bank([P, 2, HALF])
                 score_pass(sums[n, jh, mp], n, jh, mp, 0)
-        gather_words(2, 1, "res_gain1_3")
         quantise_h(1, 0)
         quantise_h(1, 1)
+        gather_words(2, 1, "h_bf1_1")
+        offered = {(jh, mp): close_e2(sums[1, jh, mp], jh, mp) for jh, mp in blocks}
         for jh, mp in blocks:
-            finish(sums[1, jh, mp], sums[2, jh, mp], jh, mp)
+            finish(offered[jh, mp], sums[2, jh, mp], jh, mp)

@@ -67,16 +67,15 @@ def tile_list_home_swap_score_kernel(
                 in_=dram_words[n][a].rearrange("p t i -> p (t i)").bitcast(I32),
             )
 
-        def load_tab_scales(a, q):
-            first = 32 * q + 4 * (1 - a)
+        def load_tab_scales(a, r):
             nc.sync.dma_start(
-                out=table_scales[0][first : first + 4, :].bitcast(I32),
-                in_=tab_scales[a, 4 * q : 4 * q + 4, :].bitcast(I32),
+                out=table_scales[0][4 * (1 - a) + r : P : 32, :].bitcast(I32),
+                in_=tab_scales[a, r:16:4, :].bitcast(I32),
             )
 
-        def load_home_scales(n, q, queue):
-            queue.dma_start(
-                out=table_scales[n][32 * q : 32 * q + 8, :].bitcast(I32),
+        def load_home_scales(n, q):
+            nc.gpsimd.dma_start(
+                out=table_scales[n][32 * q + 8 : 32 * q + 16, :].bitcast(I32),
                 in_=dram_scales[n][:, 4 * q : 4 * q + 4, :].bitcast(I32),
             )
 
@@ -100,16 +99,17 @@ def tile_list_home_swap_score_kernel(
             picked_scales[n] = sb("picked_scales%d" % n, [P, S], U8, tag)
             nc.vector.tensor_copy(picked_scales[n][:], table_scales[n][:].indirect(lists[n][:]))
 
-        for q in range(4):
-            load_home_scales(1, q, nc.gpsimd)
-        load_list(0)
-        load_list(1)
+        for n in (1, 2):
+            for q in range(4):
+                load_home_scales(n, q)
+        for n in range(3):
+            load_list(n)
         nc.sync.dma_start(out=w4_raw[:].bitcast(I32), in_=w4_words[0].bitcast(I32))
         load_w1(0)
-        for q in range(4):
+        for r in range(4):
             nc.sync.dma_start(
-                out=w4_raw_plane[32 * q : 32 * q + 4, :].bitcast(I32),
-                in_=w4_scales[0, 4 * q : 4 * q + 4, :].bitcast(I32),
+                out=w4_raw_plane[r:P:32, :].bitcast(I32),
+                in_=w4_scales[0, r:16:4, :].bitcast(I32),
             )
         load_words(0, 0)
         load_tab_scales(0, 0)
@@ -125,9 +125,6 @@ def tile_list_home_swap_score_kernel(
         load_words(1, 0)
         load_words(1, 1)
         load_res(1)
-        load_list(2)
-        for q in range(4):
-            load_home_scales(2, q, nc.sync)
         load_words(2, 0)
         load_words(2, 1)
         with nc.allow_non_contiguous_dma(reason="one scale value for each output row"):
@@ -225,7 +222,7 @@ def tile_list_home_swap_score_kernel(
                 nc.tensor.matmul_mx(
                     out=e[:, t, :],
                     lhsT=picked_words[n, a][:, rows].bitcast(FP8X4),
-                    lhsT_scale=picked_scales[n][4 * a : P, rows],
+                    lhsT_scale=picked_scales[n][8 + 4 * a : P, rows],
                     rhs=h_codes[a, jh][:].bitcast(FP8X4),
                     rhs_scale=h_plane[a][jh][:],
                     start=(a == 0 and t == 0),
@@ -259,11 +256,12 @@ def tile_list_home_swap_score_kernel(
         round_w1(0)
         w4_plane = sb("w4_plane", [P, H], U8)
         deal_columns(w4_plane, w4_raw_plane)
+        gather_scales(1, "w4_raw_plane")
         gather_words(0, 0)
         quantise_w1(0)
         round_w1(1)
         gather_scales(0)
-        gather_scales(1, "scales0")
+        gather_scales(2, "scales0")
         gather_words(0, 1)
         first_product(0)
         quantise_w1(1, "words0_1")
@@ -280,7 +278,6 @@ def tile_list_home_swap_score_kernel(
         weave_h(1, 1, nc.scalar.copy)
         quantise_h(0, 0, "tanh_x1_2")
         quantise_h(0, 1, "res_gain1_2")
-        gather_scales(2, "h_bf0_0")
         gather_words(2, 0, "h_bf0_1")
         blocks = [(jh, mp) for jh in range(2) for mp in range(2)]
         sums = {}

@@ -14,9 +14,15 @@ ACT = mybir.ActivationFunctionType
 ALU = mybir.AluOpType
 
 P = 128
+PACK = 4
+PASS = P * PACK
+BLOCKS = PASS // 32
+QUADRANT = 32
 K, H, S, T, S2, T3 = 1024, 1024, 512, 2048, 512, 1024
-PASS = 512
-HALF = 256
+HALF = S // 2
+TENANTS, HOMES, ESTATES = 0, 1, 2
+PSUM_BANKS = 8
+VECTOR_SLICES = 2
 FLOPS = 2 * K * H * S + 2 * 2 * H * S2 * S
 
 
@@ -27,7 +33,7 @@ def tile_list_home_swap_score_kernel(
     nc = tc.nc
     with ExitStack() as ctx:
         keep = ctx.enter_context(tc.tile_pool(name="keep", bufs=1))
-        psum = ctx.enter_context(tc.psum_pool(name="psum", bufs=8))
+        psum = ctx.enter_context(tc.psum_pool(name="psum", bufs=PSUM_BANKS))
 
         def sb(name, shape, dtype, tag=None):
             return keep.tile(shape, dtype, name=name, tag=tag or name, align_bytes=64)
@@ -35,122 +41,88 @@ def tile_list_home_swap_score_kernel(
         def bank(shape):
             return psum.tile(shape, F32, name="bank")
 
-        lists = [sb("list%d" % n, [P, S // 16], U16) for n in range(3)]
-        widths = [T, T3, T3]
-        table_words = [[sb("words%d_%d" % (n, a), [P, widths[n]], U32) for a in range(2)] for n in range(3)]
-        table_scales = [sb("scales%d" % n, [P, widths[n]], U8) for n in range(3)]
-        picked_words = {}
-        picked_scales = {}
-        w4_raw = sb("w4_raw", [P, H], U16)
-        w4_raw_plane = sb("w4_raw_plane", [P, H], U8)
-        w4_codes = sb("w4_codes", [P, H], U16)
-        w1_raw = [sb("w1_raw%d" % a, [P, 4, PASS], F32) for a in range(2)]
-        res_raw = [sb("res_raw%d" % a, [P, 4, S], F32) for a in range(2)]
-        gain_cols = sb("gain_cols", [P, 2, 4], F32)
-        scale_cols = sb("scale_cols", [P, S2 // P], F32)
-
-        nc.gpsimd.memset(w4_raw_plane[:].bitcast(I32), 0)
-        nc.gpsimd.memset(table_scales[1][:].bitcast(I32), 0)
-        nc.vector.memset(table_scales[0][:].bitcast(I32), 0)
-        nc.vector.memset(table_scales[2][:].bitcast(I32), 0)
-
         dram_words = [tab_words, tab2_words, tab3_words]
         dram_scales = [tab_scales, tab2_scales, tab3_scales]
         dram_lists = [offs, offs2, offs3]
+        widths = [T, T3, T3]
 
-        def load_list(n):
-            nc.sync.dma_start(lists[n][:], dram_lists[n])
+        lists = [sb("list%d" % n, [P, S // 16], U16) for n in range(3)]
+        table_scales = [sb("scales%d" % n, [P, widths[n]], U8) for n in range(3)]
+        w4_raw = sb("w4_raw", [P, H], U16)
+        w4_raw_plane = sb("w4_raw_plane", [P, H], U8)
+        w4_codes = sb("w4_codes", [P, H], U16)
+        tenant_planes = [sb("tenant_plane%d" % a, [P, S], U8) for a in range(2)]
+        pair_planes = {n: sb("pair_plane%d" % n, [P, S2], U8) for n in (HOMES, ESTATES)}
 
-        def load_words(n, a):
+        nc.gpsimd.memset(w4_raw_plane[:].bitcast(I32), 0)
+        for n in range(3):
+            nc.vector.memset(table_scales[n][QUADRANT : 2 * QUADRANT, :].bitcast(I32), 0)
+            nc.vector.memset(table_scales[n][2 * QUADRANT : P, :].bitcast(I32), 0)
+        for plane in (tenant_planes[0], tenant_planes[1], pair_planes[HOMES], pair_planes[ESTATES]):
+            nc.vector.memset(plane[:].bitcast(I32), 0)
+
+        table_words, picked_words, picked_scales = {}, {}, {}
+        w1_raw, w1_bf, w1_codes, res_raw, h_codes = {}, {}, {}, {}, {}
+
+        def load_words(n, a, tag=None):
+            table_words[n, a] = sb("words%d_%d" % (n, a), [P, widths[n]], U32, tag)
             nc.sync.dma_start(
-                out=table_words[n][a][:].bitcast(I32),
-                in_=dram_words[n][a].rearrange("p t i -> p (t i)").bitcast(I32),
+                out=table_words[n, a][:].bitcast(I32),
+                in_=dram_words[n][a].rearrange("p c i -> p (c i)").bitcast(I32),
             )
 
-        def load_tab_scales(a, r):
+        def load_scales(n):
             nc.sync.dma_start(
-                out=table_scales[0][4 * (1 - a) + r : P : 32, :].bitcast(I32),
-                in_=tab_scales[a, r:16:4, :].bitcast(I32),
+                out=table_scales[n][0 : 2 * BLOCKS, :].bitcast(I32),
+                in_=dram_scales[n].rearrange("a q c -> (a q) c").bitcast(I32),
             )
 
-        def load_home_scales(n, q):
-            nc.gpsimd.dma_start(
-                out=table_scales[n][32 * q + 8 : 32 * q + 16, :].bitcast(I32),
-                in_=dram_scales[n][:, 4 * q : 4 * q + 4, :].bitcast(I32),
+        def place_rows(queue, plane, first, n, a, r):
+            queue.dma_start(
+                out=plane[first + r : P : QUADRANT, :].bitcast(I32),
+                in_=picked_scales[n][BLOCKS * a + r : BLOCKS * (a + 1) : 4, :].bitcast(I32),
             )
 
-        def load_w1(a):
+        def load_w1(a, tag=None):
+            w1_raw[a] = sb("w1_raw%d" % a, [P, PACK, PASS], F32, tag)
             nc.sync.dma_start(
                 out=w1_raw[a][:],
-                in_=w1.rearrange("(p i) r -> p i r", i=4)[:, :, a * PASS : (a + 1) * PASS],
+                in_=w1.rearrange("(p i) r -> p i r", i=PACK)[:, :, a * PASS : (a + 1) * PASS],
             )
 
-        def load_res(a):
+        def load_res(a, tag):
+            res_raw[a] = sb("res_raw%d" % a, [P, PACK, S], F32, tag)
             nc.sync.dma_start(
                 out=res_raw[a][:],
-                in_=res[a * PASS : (a + 1) * PASS, :].rearrange("(p t) j -> p t j", t=4),
+                in_=res[a * PASS : (a + 1) * PASS, :].rearrange("(p t) j -> p t j", t=PACK),
             )
 
         def gather_words(n, a, tag=None):
             picked_words[n, a] = sb("picked%d_%d" % (n, a), [P, S], U32, tag)
-            nc.vector.tensor_copy(picked_words[n, a][:], table_words[n][a][:].indirect(lists[n][:]))
+            nc.vector.tensor_copy(picked_words[n, a][:], table_words[n, a][:].indirect(lists[n][:]))
 
-        def gather_scales(n, tag=None):
-            picked_scales[n] = sb("picked_scales%d" % n, [P, S], U8, tag)
+        def gather_scales(n):
+            picked_scales[n] = sb("picked_scales%d" % n, [P, S], U8)
             nc.vector.tensor_copy(picked_scales[n][:], table_scales[n][:].indirect(lists[n][:]))
 
-        for n in (1, 2):
-            for q in range(4):
-                load_home_scales(n, q)
-        for n in range(3):
-            load_list(n)
-        nc.sync.dma_start(out=w4_raw[:].bitcast(I32), in_=w4_words[0].bitcast(I32))
-        load_w1(0)
-        for r in range(4):
-            nc.sync.dma_start(
-                out=w4_raw_plane[r:P:32, :].bitcast(I32),
-                in_=w4_scales[0, r:16:4, :].bitcast(I32),
-            )
-        load_words(0, 0)
-        load_tab_scales(0, 0)
-        load_tab_scales(0, 1)
-        load_w1(1)
-        load_tab_scales(0, 2)
-        load_tab_scales(0, 3)
-        for q in range(4):
-            load_tab_scales(1, q)
-        load_words(0, 1)
-        load_res(0)
-        nc.sync.dma_start(out=gain_cols[:], in_=gain.rearrange("(a p t) -> p a t", a=2, t=4))
-        load_words(1, 0)
-        load_words(1, 1)
-        load_res(1)
-        load_words(2, 0)
-        load_words(2, 1)
-        with nc.allow_non_contiguous_dma(reason="one scale value for each output row"):
-            nc.sync.dma_start(out=scale_cols[:], in_=scale.rearrange("(t p) -> p t", p=P))
-
-        w1_bf = {}
-        w1_codes = {}
         w1_plane = [sb("w1_plane%d" % a, [P, PASS], U8) for a in range(2)]
-        tanh_x = [[sb("tanh_x%d_%d" % (a, t), [P, S], F32) for t in range(4)] for a in range(2)]
-        res_gain = [[sb("res_gain%d_%d" % (a, t), [P, S], F32) for t in range(4)] for a in range(2)]
-        h_planes = [sb("h_planes%d" % a, [P, 4, S], BF16) for a in range(2)]
-        h_bf = [[sb("h_bf%d_%d" % (a, jh), [P, HALF, 4], BF16) for jh in range(2)] for a in range(2)]
-        h_codes = {}
+        tanh_x = [[sb("tanh_x%d_%d" % (a, t), [P, S], F32) for t in range(PACK)] for a in range(2)]
+        res_gain = [[sb("res_gain%d_%d" % (a, t), [P, S], F32) for t in range(PACK)] for a in range(2)]
+        h_slices = [sb("h_slices%d" % a, [P, PACK, S], BF16) for a in range(2)]
+        h_woven = [[sb("h_woven%d_%d" % (a, jh), [P, HALF, PACK], BF16) for jh in range(2)] for a in range(2)]
         h_plane = [[sb("h_plane%d_%d" % (a, jh), [P, HALF], U8) for jh in range(2)] for a in range(2)]
 
         def deal_columns(dealt, raw):
             nc.vector.tensor_copy(
-                out=dealt[:].rearrange("p (a t m) -> p a t m", a=2, t=4),
-                in_=raw[:].rearrange("p (a m t) -> p a t m", a=2, t=4),
+                out=dealt[:].rearrange("p (a t m) -> p a t m", a=2, t=PACK),
+                in_=raw[:].rearrange("p (a m t) -> p a t m", a=2, t=PACK),
             )
 
         def round_w1(a):
-            w1_bf[a] = sb("w1_bf%d" % a, [P, 4, P, 4], BF16)
+            w1_bf[a] = sb("w1_bf%d" % a, [P, PACK, P, PACK], BF16)
             nc.scalar.copy(
                 out=w1_bf[a][:].rearrange("p t m i -> p m i t"),
-                in_=w1_raw[a][:].rearrange("p i (m t) -> p m i t", t=4),
+                in_=w1_raw[a][:].rearrange("p i (m t) -> p m i t", t=PACK),
             )
 
         def quantise_w1(a, tag=None):
@@ -162,16 +134,16 @@ def tile_list_home_swap_score_kernel(
             )
 
         def first_product(a):
-            for t in range(4):
-                cols = slice(t * P, (t + 1) * P)
+            for t in range(PACK):
+                w1_cols = slice(t * P, (t + 1) * P)
                 w4_cols = slice(a * PASS + t * P, a * PASS + (t + 1) * P)
                 x = bank([P, S])
                 nc.tensor.matmul_mx(
                     out=x[:],
-                    lhsT=w1_codes[a][:, cols].bitcast(FP8X4),
-                    lhsT_scale=w1_plane[a][:, cols],
-                    rhs=picked_words[0, 0][:].bitcast(FP8X4),
-                    rhs_scale=picked_scales[0][4:P, :],
+                    lhsT=w1_codes[a][:, w1_cols].bitcast(FP8X4),
+                    lhsT_scale=w1_plane[a][:, w1_cols],
+                    rhs=picked_words[TENANTS, 0][:].bitcast(FP8X4),
+                    rhs_scale=tenant_planes[0][:],
                     start=True,
                     stop=False,
                 )
@@ -179,16 +151,16 @@ def tile_list_home_swap_score_kernel(
                     out=x[:],
                     lhsT=w4_codes[:, w4_cols].bitcast(FP4X4),
                     lhsT_scale=w4_plane[:, w4_cols],
-                    rhs=picked_words[0, 1][:].bitcast(FP8X4),
-                    rhs_scale=picked_scales[0][:],
+                    rhs=picked_words[TENANTS, 1][:].bitcast(FP8X4),
+                    rhs_scale=tenant_planes[1][:],
                     start=False,
                     stop=True,
                 )
                 nc.scalar.activation(out=tanh_x[a][t][:], in_=x[:], func=ACT.Tanh)
 
-        def scale_res(a, vector_planes):
-            for t in range(4):
-                if t < vector_planes:
+        def scale_res(a, vector_slices):
+            for t in range(PACK):
+                if t < vector_slices:
                     nc.vector.tensor_scalar_mul(res_gain[a][t][:], res_raw[a][:, t, :], gain_cols[:, a, t : t + 1])
                 else:
                     nc.scalar.activation(
@@ -196,16 +168,16 @@ def tile_list_home_swap_score_kernel(
                     )
 
         def make_h(a):
-            for t in range(4):
+            for t in range(PACK):
                 nc.vector.scalar_tensor_tensor(
-                    out=h_planes[a][:, t, :], in0=tanh_x[a][t][:], scalar=gain_cols[:, a, t : t + 1],
+                    out=h_slices[a][:, t, :], in0=tanh_x[a][t][:], scalar=gain_cols[:, a, t : t + 1],
                     in1=res_gain[a][t][:], op0=ALU.mult, op1=ALU.add,
                 )
 
-        def weave_h(a, jh, copy):
-            copy(
-                out=h_bf[a][jh][:].rearrange("p (g n) t -> p g t n", n=4),
-                in_=h_planes[a][:, :, jh * HALF : (jh + 1) * HALF].rearrange("p t (g n) -> p g t n", n=4),
+        def weave_h(a, jh):
+            nc.scalar.copy(
+                out=h_woven[a][jh][:].rearrange("p (g n) t -> p g t n", n=4),
+                in_=h_slices[a][:, :, jh * HALF : (jh + 1) * HALF].rearrange("p t (g n) -> p g t n", n=4),
             )
 
         def quantise_h(a, jh, tag=None):
@@ -213,30 +185,30 @@ def tile_list_home_swap_score_kernel(
             nc.vector.quantize_mx(
                 out=h_codes[a, jh][:].bitcast(FP8X4),
                 scales=h_plane[a][jh][:],
-                in_=h_bf[a][jh][:].rearrange("p j t -> p (j t)"),
+                in_=h_woven[a][jh][:].rearrange("p j t -> p (j t)"),
             )
 
         def score_pass(e, n, jh, mp, a):
-            for t in range(2):
-                rows = slice((2 * mp + t) * P, (2 * mp + t + 1) * P)
+            for mt in range(2):
+                candidates = slice((2 * mp + mt) * P, (2 * mp + mt + 1) * P)
                 nc.tensor.matmul_mx(
-                    out=e[:, t, :],
-                    lhsT=picked_words[n, a][:, rows].bitcast(FP8X4),
-                    lhsT_scale=picked_scales[n][8 + 4 * a : P, rows],
+                    out=e[:, mt, :],
+                    lhsT=picked_words[n, a][:, candidates].bitcast(FP8X4),
+                    lhsT_scale=pair_planes[n][4 * a : P, candidates],
                     rhs=h_codes[a, jh][:].bitcast(FP8X4),
                     rhs_scale=h_plane[a][jh][:],
-                    start=(a == 0 and t == 0),
-                    stop=(a == 1 and t == 1),
+                    start=(a == 0 and mt == 0),
+                    stop=(a == 1 and mt == 1),
                 )
 
         def close_e2(e2, jh, mp):
-            score_pass(e2, 1, jh, mp, 1)
+            score_pass(e2, HOMES, jh, mp, 1)
             e2_sb = sb("e2_sb%d_%d" % (jh, mp), [P, 2, HALF], F32)
             nc.scalar.copy(out=e2_sb[:], in_=e2[:])
             return e2_sb
 
         def finish(e2_sb, e3, jh, mp):
-            score_pass(e3, 2, jh, mp, 1)
+            score_pass(e3, ESTATES, jh, mp, 1)
             larger = sb("larger%d_%d" % (jh, mp), [P, 2, HALF], F32)
             nc.vector.tensor_tensor(out=larger[:], in0=e3[:], in1=e2_sb[:], op=ALU.max)
             result = sb("result%d_%d" % (jh, mp), [P, 2, HALF], F32)
@@ -248,46 +220,84 @@ def tile_list_home_swap_score_kernel(
                 scalar1=scale_cols[:, 2 * mp + 1 : 2 * mp + 2], scalar2=0.0, op0=ALU.mult, op1=ALU.add,
             )
             nc.sync.dma_start(
-                out=out[2 * mp * P : 2 * (mp + 1) * P, jh * HALF : (jh + 1) * HALF].rearrange("(t p) j -> p t j", p=P),
+                out=out[2 * mp * P : 2 * (mp + 1) * P, jh * HALF : (jh + 1) * HALF].rearrange("(mt p) j -> p mt j", p=P),
                 in_=result[:],
             )
 
+        gain_cols = sb("gain_cols", [P, 2, PACK], F32)
+        nc.gpsimd.dma_start(out=gain_cols[:], in_=gain.rearrange("(a p t) -> p a t", a=2, t=PACK))
+        for n in range(3):
+            nc.sync.dma_start(lists[n][:], dram_lists[n])
+            load_scales(n)
+        nc.sync.dma_start(out=w4_raw[:].bitcast(I32), in_=w4_words[0].bitcast(I32))
+        load_w1(0)
+        for r in range(4):
+            nc.sync.dma_start(
+                out=w4_raw_plane[r:P:QUADRANT, :].bitcast(I32),
+                in_=w4_scales[0, r:BLOCKS:4, :].bitcast(I32),
+            )
+        load_words(TENANTS, 0)
+        for n in range(3):
+            gather_scales(n)
         deal_columns(w4_codes, w4_raw)
         round_w1(0)
         w4_plane = sb("w4_plane", [P, H], U8)
         deal_columns(w4_plane, w4_raw_plane)
-        gather_scales(1, "w4_raw_plane")
-        gather_words(0, 0)
+        gather_words(TENANTS, 0)
         quantise_w1(0)
+
+        load_w1(1, "scales0")
+        for r in range(4):
+            place_rows(nc.sync, tenant_planes[0], 0, TENANTS, 0, r)
+        place_rows(nc.sync, tenant_planes[1], 0, TENANTS, 1, 0)
+        load_words(TENANTS, 1, "scales1")
+        for r in range(1, 4):
+            place_rows(nc.gpsimd, tenant_planes[1], 0, TENANTS, 1, r)
+        row_groups = [(a, r) for a in range(2) for r in range(4)]
+        for a, r in row_groups:
+            place_rows(nc.gpsimd, pair_planes[ESTATES], 4 * a, ESTATES, a, r)
         round_w1(1)
-        gather_scales(0)
-        gather_scales(2, "scales0")
-        gather_words(0, 1)
+        load_res(0, "scales2")
+        load_words(HOMES, 0, "w4_raw")
+        load_words(HOMES, 1, "w1_raw0")
+        for a, r in row_groups[:2]:
+            place_rows(nc.sync, pair_planes[HOMES], 4 * a, HOMES, a, r)
+        load_res(1, "words0_0")
+        for a, r in row_groups[2:]:
+            place_rows(nc.sync, pair_planes[HOMES], 4 * a, HOMES, a, r)
+        load_words(ESTATES, 0, "w4_raw_plane")
+        load_words(ESTATES, 1, "scales0")
+
+        gather_words(TENANTS, 1)
         first_product(0)
-        quantise_w1(1, "words0_1")
+        quantise_w1(1, "scales1")
         first_product(1)
-        scale_res(0, 4)
+        scale_res(0, PACK)
         make_h(0)
-        scale_res(1, 2)
-        weave_h(0, 0, nc.scalar.copy)
-        weave_h(0, 1, nc.scalar.copy)
-        gather_words(1, 0)
-        gather_words(1, 1)
+        scale_res(1, VECTOR_SLICES)
+        weave_h(0, 0)
+        weave_h(0, 1)
+        gather_words(HOMES, 0)
+        gather_words(HOMES, 1)
+        scale_cols = sb("scale_cols", [P, S2 // P], F32, "w4_raw")
+        with nc.allow_non_contiguous_dma(reason="one scale value for each output row"):
+            nc.sync.dma_start(out=scale_cols[:], in_=scale.rearrange("(c p) -> p c", p=P))
         make_h(1)
-        weave_h(1, 0, nc.scalar.copy)
-        weave_h(1, 1, nc.scalar.copy)
+        weave_h(1, 0)
+        weave_h(1, 1)
+
         quantise_h(0, 0, "tanh_x1_2")
         quantise_h(0, 1, "res_gain1_2")
-        gather_words(2, 0, "h_bf0_1")
+        gather_words(ESTATES, 0, "h_woven0_1")
         blocks = [(jh, mp) for jh in range(2) for mp in range(2)]
         sums = {}
-        for n in (1, 2):
+        for n in (HOMES, ESTATES):
             for jh, mp in blocks:
                 sums[n, jh, mp] = bank([P, 2, HALF])
                 score_pass(sums[n, jh, mp], n, jh, mp, 0)
         quantise_h(1, 0)
         quantise_h(1, 1)
-        gather_words(2, 1, "h_bf1_1")
-        offered = {(jh, mp): close_e2(sums[1, jh, mp], jh, mp) for jh, mp in blocks}
+        gather_words(ESTATES, 1, "h_woven1_1")
+        e2_in_sbuf = {(jh, mp): close_e2(sums[HOMES, jh, mp], jh, mp) for jh, mp in blocks}
         for jh, mp in blocks:
-            finish(offered[jh, mp], sums[2, jh, mp], jh, mp)
+            finish(e2_in_sbuf[jh, mp], sums[ESTATES, jh, mp], jh, mp)

from contextlib import ExitStack

import concourse.mybir as mybir

F32 = mybir.dt.float32
BF16 = mybir.dt.bfloat16
I32 = mybir.dt.int32
U32 = mybir.dt.uint32
U16 = mybir.dt.uint16
U8 = mybir.dt.uint8
FP8X4 = mybir.dt.float8_e4m3fn_x4
FP4X4 = mybir.dt.float4_e2m1fn_x4
ACT = mybir.ActivationFunctionType
ALU = mybir.AluOpType

P = 128
PACK = 4
PASS = P * PACK
BLOCKS = PASS // 32
QUADRANT = 32
K, H, S, T, S2, T3 = 1024, 1024, 512, 2048, 512, 1024
HALF = S // 2
TENANTS, HOMES, ESTATES = 0, 1, 2
PSUM_BANKS = 8
VECTOR_SLICES = 2
FLOPS = 2 * K * H * S + 2 * 2 * H * S2 * S


def tile_list_home_swap_score_kernel(
    tc, tab_words, tab_scales, offs, tab2_words, tab2_scales, offs2, tab3_words, tab3_scales, offs3,
    w1, w4_words, w4_scales, res, gain, scale, out,
):
    nc = tc.nc
    with ExitStack() as ctx:
        keep = ctx.enter_context(tc.tile_pool(name="keep", bufs=1))
        psum = ctx.enter_context(tc.psum_pool(name="psum", bufs=PSUM_BANKS))

        def sb(name, shape, dtype, tag=None):
            return keep.tile(shape, dtype, name=name, tag=tag or name, align_bytes=64)

        def bank(shape):
            return psum.tile(shape, F32, name="bank")

        dram_words = [tab_words, tab2_words, tab3_words]
        dram_scales = [tab_scales, tab2_scales, tab3_scales]
        dram_lists = [offs, offs2, offs3]
        widths = [T, T3, T3]

        lists = [sb("list%d" % n, [P, S // 16], U16) for n in range(3)]
        table_scales = [sb("scales%d" % n, [P, widths[n]], U8) for n in range(3)]
        w4_raw = sb("w4_raw", [P, H], U16)
        w4_raw_plane = sb("w4_raw_plane", [P, H], U8)
        w4_codes = sb("w4_codes", [P, H], U16)
        tenant_planes = [sb("tenant_plane%d" % a, [P, S], U8) for a in range(2)]
        pair_planes = {n: sb("pair_plane%d" % n, [P, S2], U8) for n in (HOMES, ESTATES)}

        nc.gpsimd.memset(w4_raw_plane[:].bitcast(I32), 0)
        for n in range(3):
            nc.vector.memset(table_scales[n][QUADRANT : 2 * QUADRANT, :].bitcast(I32), 0)
            nc.vector.memset(table_scales[n][2 * QUADRANT : P, :].bitcast(I32), 0)
        for plane in (tenant_planes[0], tenant_planes[1], pair_planes[HOMES], pair_planes[ESTATES]):
            nc.vector.memset(plane[:].bitcast(I32), 0)

        table_words, picked_words, picked_scales = {}, {}, {}
        w1_raw, w1_bf, w1_codes, res_raw, h_codes = {}, {}, {}, {}, {}

        def load_words(n, a, tag=None):
            table_words[n, a] = sb("words%d_%d" % (n, a), [P, widths[n]], U32, tag)
            nc.sync.dma_start(
                out=table_words[n, a][:].bitcast(I32),
                in_=dram_words[n][a].rearrange("p c i -> p (c i)").bitcast(I32),
            )

        def load_scales(n):
            nc.sync.dma_start(
                out=table_scales[n][0 : 2 * BLOCKS, :].bitcast(I32),
                in_=dram_scales[n].rearrange("a q c -> (a q) c").bitcast(I32),
            )

        def place_rows(queue, plane, first, n, a, r):
            queue.dma_start(
                out=plane[first + r : P : QUADRANT, :].bitcast(I32),
                in_=picked_scales[n][BLOCKS * a + r : BLOCKS * (a + 1) : 4, :].bitcast(I32),
            )

        def load_w1(a, tag=None):
            w1_raw[a] = sb("w1_raw%d" % a, [P, PACK, PASS], F32, tag)
            nc.sync.dma_start(
                out=w1_raw[a][:],
                in_=w1.rearrange("(p i) r -> p i r", i=PACK)[:, :, a * PASS : (a + 1) * PASS],
            )

        def load_res(a, tag):
            res_raw[a] = sb("res_raw%d" % a, [P, PACK, S], F32, tag)
            nc.sync.dma_start(
                out=res_raw[a][:],
                in_=res[a * PASS : (a + 1) * PASS, :].rearrange("(p t) j -> p t j", t=PACK),
            )

        def gather_words(n, a, tag=None):
            picked_words[n, a] = sb("picked%d_%d" % (n, a), [P, S], U32, tag)
            nc.vector.tensor_copy(picked_words[n, a][:], table_words[n, a][:].indirect(lists[n][:]))

        def gather_scales(n):
            picked_scales[n] = sb("picked_scales%d" % n, [P, S], U8)
            nc.vector.tensor_copy(picked_scales[n][:], table_scales[n][:].indirect(lists[n][:]))

        w1_plane = [sb("w1_plane%d" % a, [P, PASS], U8) for a in range(2)]
        tanh_x = [[sb("tanh_x%d_%d" % (a, t), [P, S], F32) for t in range(PACK)] for a in range(2)]
        res_gain = [[sb("res_gain%d_%d" % (a, t), [P, S], F32) for t in range(PACK)] for a in range(2)]
        h_slices = [sb("h_slices%d" % a, [P, PACK, S], BF16) for a in range(2)]
        h_woven = [[sb("h_woven%d_%d" % (a, jh), [P, HALF, PACK], BF16) for jh in range(2)] for a in range(2)]
        h_plane = [[sb("h_plane%d_%d" % (a, jh), [P, HALF], U8) for jh in range(2)] for a in range(2)]

        def deal_columns(dealt, raw):
            nc.vector.tensor_copy(
                out=dealt[:].rearrange("p (a t m) -> p a t m", a=2, t=PACK),
                in_=raw[:].rearrange("p (a m t) -> p a t m", a=2, t=PACK),
            )

        def round_w1(a):
            w1_bf[a] = sb("w1_bf%d" % a, [P, PACK, P, PACK], BF16)
            nc.scalar.copy(
                out=w1_bf[a][:].rearrange("p t m i -> p m i t"),
                in_=w1_raw[a][:].rearrange("p i (m t) -> p m i t", t=PACK),
            )

        def quantise_w1(a, tag=None):
            w1_codes[a] = sb("w1_codes%d" % a, [P, PASS], U32, tag)
            nc.vector.quantize_mx(
                out=w1_codes[a][:].bitcast(FP8X4),
                scales=w1_plane[a][:],
                in_=w1_bf[a][:].rearrange("p t m i -> p (t m i)"),
            )

        def first_product(a):
            for t in range(PACK):
                w1_cols = slice(t * P, (t + 1) * P)
                w4_cols = slice(a * PASS + t * P, a * PASS + (t + 1) * P)
                x = bank([P, S])
                nc.tensor.matmul_mx(
                    out=x[:],
                    lhsT=w1_codes[a][:, w1_cols].bitcast(FP8X4),
                    lhsT_scale=w1_plane[a][:, w1_cols],
                    rhs=picked_words[TENANTS, 0][:].bitcast(FP8X4),
                    rhs_scale=tenant_planes[0][:],
                    start=True,
                    stop=False,
                )
                nc.tensor.matmul_mx(
                    out=x[:],
                    lhsT=w4_codes[:, w4_cols].bitcast(FP4X4),
                    lhsT_scale=w4_plane[:, w4_cols],
                    rhs=picked_words[TENANTS, 1][:].bitcast(FP8X4),
                    rhs_scale=tenant_planes[1][:],
                    start=False,
                    stop=True,
                )
                nc.scalar.activation(out=tanh_x[a][t][:], in_=x[:], func=ACT.Tanh)

        def scale_res(a, vector_slices):
            for t in range(PACK):
                if t < vector_slices:
                    nc.vector.tensor_scalar_mul(res_gain[a][t][:], res_raw[a][:, t, :], gain_cols[:, a, t : t + 1])
                else:
                    nc.scalar.activation(
                        out=res_gain[a][t][:], in_=res_raw[a][:, t, :], func=ACT.Copy, scale=gain_cols[:, a, t : t + 1]
                    )

        def make_h(a):
            for t in range(PACK):
                nc.vector.scalar_tensor_tensor(
                    out=h_slices[a][:, t, :], in0=tanh_x[a][t][:], scalar=gain_cols[:, a, t : t + 1],
                    in1=res_gain[a][t][:], op0=ALU.mult, op1=ALU.add,
                )

        def weave_h(a, jh):
            nc.scalar.copy(
                out=h_woven[a][jh][:].rearrange("p (g n) t -> p g t n", n=4),
                in_=h_slices[a][:, :, jh * HALF : (jh + 1) * HALF].rearrange("p t (g n) -> p g t n", n=4),
            )

        def quantise_h(a, jh, tag=None):
            h_codes[a, jh] = sb("h_codes%d_%d" % (a, jh), [P, HALF], U32, tag)
            nc.vector.quantize_mx(
                out=h_codes[a, jh][:].bitcast(FP8X4),
                scales=h_plane[a][jh][:],
                in_=h_woven[a][jh][:].rearrange("p j t -> p (j t)"),
            )

        def score_pass(e, n, jh, mp, a):
            for mt in range(2):
                candidates = slice((2 * mp + mt) * P, (2 * mp + mt + 1) * P)
                nc.tensor.matmul_mx(
                    out=e[:, mt, :],
                    lhsT=picked_words[n, a][:, candidates].bitcast(FP8X4),
                    lhsT_scale=pair_planes[n][4 * a : P, candidates],
                    rhs=h_codes[a, jh][:].bitcast(FP8X4),
                    rhs_scale=h_plane[a][jh][:],
                    start=(a == 0 and mt == 0),
                    stop=(a == 1 and mt == 1),
                )

        def close_e2(e2, jh, mp):
            score_pass(e2, HOMES, jh, mp, 1)
            e2_sb = sb("e2_sb%d_%d" % (jh, mp), [P, 2, HALF], F32)
            nc.scalar.copy(out=e2_sb[:], in_=e2[:])
            return e2_sb

        def finish(e2_sb, e3, jh, mp):
            score_pass(e3, ESTATES, jh, mp, 1)
            larger = sb("larger%d_%d" % (jh, mp), [P, 2, HALF], F32)
            nc.vector.tensor_tensor(out=larger[:], in0=e3[:], in1=e2_sb[:], op=ALU.max)
            result = sb("result%d_%d" % (jh, mp), [P, 2, HALF], F32)
            nc.scalar.activation(
                out=result[:, 0, :], in_=larger[:, 0, :], func=ACT.Copy, scale=scale_cols[:, 2 * mp : 2 * mp + 1]
            )
            nc.gpsimd.tensor_scalar(
                out=result[:, 1, :], in0=larger[:, 1, :],
                scalar1=scale_cols[:, 2 * mp + 1 : 2 * mp + 2], scalar2=0.0, op0=ALU.mult, op1=ALU.add,
            )
            nc.sync.dma_start(
                out=out[2 * mp * P : 2 * (mp + 1) * P, jh * HALF : (jh + 1) * HALF].rearrange("(mt p) j -> p mt j", p=P),
                in_=result[:],
            )

        gain_cols = sb("gain_cols", [P, 2, PACK], F32)
        nc.gpsimd.dma_start(out=gain_cols[:], in_=gain.rearrange("(a p t) -> p a t", a=2, t=PACK))
        for n in range(3):
            nc.sync.dma_start(lists[n][:], dram_lists[n])
            load_scales(n)
        nc.sync.dma_start(out=w4_raw[:].bitcast(I32), in_=w4_words[0].bitcast(I32))
        load_w1(0)
        for r in range(4):
            nc.sync.dma_start(
                out=w4_raw_plane[r:P:QUADRANT, :].bitcast(I32),
                in_=w4_scales[0, r:BLOCKS:4, :].bitcast(I32),
            )
        load_words(TENANTS, 0)
        for n in range(3):
            gather_scales(n)
        deal_columns(w4_codes, w4_raw)
        round_w1(0)
        w4_plane = sb("w4_plane", [P, H], U8)
        deal_columns(w4_plane, w4_raw_plane)
        gather_words(TENANTS, 0)
        quantise_w1(0)

        load_w1(1, "scales0")
        for r in range(4):
            place_rows(nc.sync, tenant_planes[0], 0, TENANTS, 0, r)
        place_rows(nc.sync, tenant_planes[1], 0, TENANTS, 1, 0)
        load_words(TENANTS, 1, "scales1")
        for r in range(1, 4):
            place_rows(nc.gpsimd, tenant_planes[1], 0, TENANTS, 1, r)
        row_groups = [(a, r) for a in range(2) for r in range(4)]
        for a, r in row_groups:
            place_rows(nc.gpsimd, pair_planes[ESTATES], 4 * a, ESTATES, a, r)
        round_w1(1)
        load_res(0, "scales2")
        load_words(HOMES, 0, "w4_raw")
        load_words(HOMES, 1, "w1_raw0")
        for a, r in row_groups[:2]:
            place_rows(nc.sync, pair_planes[HOMES], 4 * a, HOMES, a, r)
        load_res(1, "words0_0")
        for a, r in row_groups[2:]:
            place_rows(nc.sync, pair_planes[HOMES], 4 * a, HOMES, a, r)
        load_words(ESTATES, 0, "w4_raw_plane")
        load_words(ESTATES, 1, "scales0")

        gather_words(TENANTS, 1)
        first_product(0)
        quantise_w1(1, "scales1")
        first_product(1)
        scale_res(0, PACK)
        make_h(0)
        scale_res(1, VECTOR_SLICES)
        weave_h(0, 0)
        weave_h(0, 1)
        gather_words(HOMES, 0)
        gather_words(HOMES, 1)
        scale_cols = sb("scale_cols", [P, S2 // P], F32, "w4_raw")
        with nc.allow_non_contiguous_dma(reason="one scale value for each output row"):
            nc.sync.dma_start(out=scale_cols[:], in_=scale.rearrange("(c p) -> p c", p=P))
        make_h(1)
        weave_h(1, 0)
        weave_h(1, 1)

        quantise_h(0, 0, "tanh_x1_2")
        quantise_h(0, 1, "res_gain1_2")
        gather_words(ESTATES, 0, "h_woven0_1")
        blocks = [(jh, mp) for jh in range(2) for mp in range(2)]
        sums = {}
        for n in (HOMES, ESTATES):
            for jh, mp in blocks:
                sums[n, jh, mp] = bank([P, 2, HALF])
                score_pass(sums[n, jh, mp], n, jh, mp, 0)
        quantise_h(1, 0)
        quantise_h(1, 1)
        gather_words(ESTATES, 1, "h_woven1_1")
        e2_in_sbuf = {(jh, mp): close_e2(sums[HOMES, jh, mp], jh, mp) for jh, mp in blocks}
        for jh, mp in blocks:
            finish(e2_in_sbuf[jh, mp], sums[ESTATES, jh, mp], jh, mp)
